import numpy as np, ml_dtypes
CORES = [16,23,24,31,64,71]
N = 6
import mx_ref
NC = 256
C2 = np.float32(0.30933)
BF = ml_dtypes.bfloat16
def cut(t, i, w=512):
    return t[:, w * i:w * i + w]
def tile(rs):
    return np.stack(rs, axis=2).reshape(128, -1).astype(BF)
def pick(b):
    s = np.zeros((128, 128, 4), np.float32)
    s[np.arange(128), np.arange(128), b] = 1.0
    return mx_ref.quantize(s.reshape(128, 512).astype(BF))
def setup_inputs(rng):
    def f(*shape):
        return mx_ref.flush((rng.standard_normal(shape, dtype=np.float32) * np.exp2(rng.integers(-2, 3, shape[:-1] + (1,)))).astype(BF))
    return {"b": f(N, 128, N * 512), "x": f(N, 128, 4 * NC)}
def setup_inputs_blocks(rng):
    d = setup_inputs(rng)
    for k in ("b", "x"): d[k] = mx_ref.spread(d[k], rng, 2)
    return d
def setup_inputs_wide(rng):
    d = setup_inputs(rng)
    for k in ("b", "x"): d[k] = mx_ref.flush((d[k].astype(np.float32) * np.exp2(rng.integers(-4, 5, (N, 1, 1))).astype(np.float32)).astype(BF))
    return d
def reference(b, x, own=None):
    S = [pick(t) for t in range(4)]
    h = np.zeros((N, 128, 512), BF)
    for c in range(N):
        for r in range(N):
            q = mx_ref.quantize(cut(b[r], c))
            P = [mx_ref.matmul(S[t], q) for t in range(4)]
            Z = P if r == 0 else [z + p for z, p in zip(Z, P)]
        h[c] = tile([np.maximum(Z[t], 0) * C2 for t in range(4)])
    use = h if own is None else own["h"]
    H = [mx_ref.quantize(use[j]) for j in range(N)]
    y = np.zeros((N, 128, N * NC), np.float32)
    for r in range(N):
        qx = mx_ref.quantize(x[r])
        for j in range(N):
            y[r][:, NC * j:NC * j + NC] = mx_ref.matmul(H[j], qx)
    return {"h": h, "y": y}

@@ -1,0 +1,257 @@
+from concourse.bass import DstId, RemoteDMATransfer
+from concourse.mybir import dt, AluOpType, ActivationFunctionType
+
+N = 6
+SIM = 80
+W = 128
+NX = 256
+C2 = 0.30933
+CODES = "float8_e4m3fn_x4"
+
+SCRATCH = {
+    "bt": ("sbuf", [128, N * 4 * W], "bfloat16"),
+    "xt": ("sbuf", [128, 4 * NX], "bfloat16"),
+    "bc": ("sbuf", [128, N * W], CODES),
+    "bp": ("sbuf", [128, N * W], "uint8"),
+    "xc": ("sbuf", [128, NX], CODES),
+    "xp": ("sbuf", [128, NX], "uint8"),
+    "one": ("sbuf", [128, W], "bfloat16"),
+    "eye": ("sbuf", [128, 4 * W + 4], "bfloat16"),
+    "sc": ("sbuf", [128, 4 * W], CODES),
+    "sp": ("sbuf", [128, 4 * W], "uint8"),
+    "l1c": ("sbuf", [128, N * W], CODES),
+    "l1p": ("sbuf", [128, N * W], "uint8"),
+    "l2c": ("sbuf", [128, N * W], CODES),
+    "l2p": ("sbuf", [128, N * W], "uint8"),
+    "r1c": ("sbuf", [128, N * W], CODES),
+    "r1p": ("sbuf", [128, N * W], "uint8"),
+    "r2c": ("sbuf", [128, W], CODES),
+    "r2p": ("sbuf", [128, W], "uint8"),
+    "ht": ("sbuf", [128, 4 * W], "bfloat16"),
+    "hc": ("sbuf", [128, W], CODES),
+    "hp": ("sbuf", [128, W], "uint8"),
+    "yo": ("sbuf", [128, N * NX], "float32"),
+    "zb": ("psum", [128, 2048], "float32"),
+    "yb": ("psum", [128, 2048], "float32"),
+}
+SEMAPHORES = (["a1_%d" % r for r in range(N)] + ["a2_%d" % r for r in range(N)] + ["r1c", "r1p", "r2c", "r2p", "sent"]
+              + ["ld%d" % k for k in range(N)] + ["bq%d" % k for k in range(N)] + ["ldx", "xq", "ones", "eye", "sq"]
+              + ["z%d" % b for b in range(4)] + ["rv", "rs", "hq"]
+              + ["y%d" % k for k in range(N)] + ["e%d" % k for k in range(N)] + ["st_y", "st_a"])
+
+
+def engines(mask):
+    return [e for e in range(mask.bit_length()) if mask >> e & 1]
+
+
+def far(s, d, topo):
+    a, b = topo.chip(s), topo.chip(d)
+    k = 0 if a == b else 1 if topo.mates(a, b) else 2 if topo.same_plane(a, b) else 3
+    return k + (0 if topo.may_write(s, d) else 4)
+
+
+def chip_groups(me, cores, topo):
+    out = []
+    for r, c in enumerate(cores):
+        if out and topo.chip(cores[out[-1][-1]]) == topo.chip(c):
+            out[-1].append(r)
+        else:
+            out.append([r])
+    return sorted(out, key=lambda q: 0 if me in q else -max(far(cores[me], cores[r], topo) for r in q))
+
+
+def relays(s, cores, topo):
+    barred = [r for r, d in enumerate(cores) if d != s and not topo.may_write(s, d)]
+    if not barred:
+        return []
+    barred.sort(key=lambda r: (-far(s, cores[r], topo), r))
+    near = [h for h in range(SIM) if topo.chip(h) == topo.chip(s) and topo.die(h) == topo.die(s)
+            and h not in cores and all(topo.may_write(h, cores[r]) for r in barred)]
+    per = -(-len(barred) // len(near))
+    return [(h, barred[per * i:per * i + per]) for i, h in enumerate(near) if per * i < len(barred)]
+
+
+def plan(cores, topo):
+    steps = {}
+
+    def call(core, waits, transfers):
+        steps.setdefault(core, []).append((waits, transfers))
+
+    for me, s in enumerate(cores):
+        rel = relays(s, cores, topo)
+        served = [r for _, rs in rel for r in rs]
+        peers = [r for r, d in enumerate(cores) if d != s and topo.chip(d) == topo.chip(s)]
+        direct = [r for r, d in enumerate(cores) if d != s and r not in served and r not in peers]
+        out = engines(topo.mask(s, [d for d in cores if topo.chip(d) != topo.chip(s)][0]))
+        here = [e for e in engines(topo.mask(s, cores[peers[0]])) if e not in out]
+        gs = chip_groups(me, cores, topo)
+        bq = {r: "bq%d" % k for k, q in enumerate(gs) for r in q}
+
+        def spread(ranks, en):
+            return [([r], cores[r], r, en[i::len(ranks)]) for i, r in enumerate(ranks)]
+
+        if rel:
+            first = [(rs, h, None, here[i::len(rel)]) for i, (h, rs) in enumerate(rel)]
+            rest = spread(direct, out) + spread(peers, here)
+        else:
+            first = spread(gs[0], out)
+            rest = spread([r for r in direct if r not in gs[0]], out) + spread(peers, here[::2])
+        for part in (first, rest):
+            for kind in "cp":
+                waits = sorted(set(bq[r] for rs, _, _, _ in part for r in rs))
+                tr = []
+                for rs, d, r, en in part:
+                    a, b = W * rs[0], W * rs[-1] + W
+                    if r is None:
+                        tr.append((("b" + kind, a, b), [(d, "r1" + kind, 0, b - a)], en, "r1" + kind))
+                    else:
+                        tr.append((("b" + kind, a, b), [(d, "l1" + kind, W * me, W * me + W)], en, "a1_%d" % me))
+                call(s, waits, tr)
+
+        def to(ranks, kind, en):
+            return (("h" + kind, 0, W), [(cores[r], "l2" + kind, W * me, W * me + W) for r in ranks], en, "a2_%d" % me)
+
+        for kind in "cp":
+            if rel:
+                tr = [(("h" + kind, 0, W), [(h, "r2" + kind, 0, W) for h, _ in rel], here, "r2" + kind)]
+            else:
+                tr = [to(peers, kind, here[::2])]
+            if direct:
+                tr.append(to(sorted(direct, key=lambda r: -far(s, cores[r], topo)), kind, out))
+            call(s, ["hq"], tr)
+        if rel:
+            for kind in "cp":
+                call(s, ["hq"], [to(peers, kind, here)])
+
+        for h, rs in rel:
+            use = out if len(rs) > 1 else out[::2]
+            for kind in "cp":
+                call(h, ["r1" + kind], [(("r1" + kind, W * i, W * i + W), [(cores[r], "l1" + kind, W * me, W * me + W)],
+                                         use[i::len(rs)], "a1_%d" % me) for i, r in enumerate(rs)])
+            for kind in "cp":
+                call(h, ["r2" + kind], [(("r2" + kind, 0, W), [(cores[r], "l2" + kind, W * me, W * me + W) for r in rs],
+                                         use, "a2_%d" % me)])
+    return steps
+
+
+def landed(steps, core, sem):
+    return sum(len(en) for calls in steps.values() for _, tr in calls for _, dsts, en, name in tr
+               for d in dsts if d[0] == core and name == sem)
+
+
+def side(T, buf, a, b):
+    ap = T[buf][:, a:b]
+    return ap.bitcast(dt.uint8) if buf[-1] == "c" else ap
+
+
+def remote_calls(g, core, T, topo, steps):
+    total = 0
+    for waits, tr in steps[core]:
+        for w in waits:
+            g.wait_ge(T.sem[w], landed(steps, core, w) if w[0] == "r" else 1)
+        xs = []
+        for (buf, a, b), dsts, en, name in tr:
+            ids = [topo.addr(d[0]) for d in dsts]
+            xs.append(RemoteDMATransfer(srcs=[side(T, buf, a, b)], dsts=[side(T, d[1], d[2], d[3]) for d in dsts],
+                                        dst_ids=[DstId(rid=i[0], pnc=i[1]) for i in ids],
+                                        dma_engine_mask=sum(1 << e for e in en), remote_sem=T.sem[name]))
+            total += len(en)
+        g.remote_dma_fused(xs, local_sem=T.sem.sent)
+    g.wait_ge(T.sem.sent, total)
+
+
+def rank_program(g, core, T, topo):
+    cores = list(T.cores)
+    steps = plan(cores, topo)
+    if core not in steps:
+        return
+    me = T.rank_of(core)
+    if me is None:
+        remote_calls(g, core, T, topo, steps)
+        return
+
+    gs = chip_groups(me, cores, topo)
+    bq = {r: "bq%d" % k for k, q in enumerate(gs) for r in q}
+    order = sorted([r for r in range(N) if r != me], key=lambda r: (far(cores[r], core, topo), r))
+    seq = [me] + order
+    sem = T.sem
+
+    for k, q in enumerate(gs):
+        a, b = 4 * W * q[0], 4 * W * q[-1] + 4 * W
+        g.sync.dma_start(T.bt[0:64, a:b], T.b[0:64, a:b]).then_inc(sem["ld%d" % k], 16)
+        g.scalar.dma_start(T.bt[64:128, a:b], T.b[64:128, a:b]).then_inc(sem["ld%d" % k], 16)
+    g.sync.dma_start(T.xt[:], T.x[:]).then_inc(sem.ldx, 16)
+
+    v = g.vector
+    v.memset(T.one[:], 1.0).then_inc(sem.ones, 1)
+    v.memset(T.eye[:], 0.0).then_inc(sem.ones, 1)
+    for k, q in enumerate(gs):
+        a, b = W * q[0], W * q[-1] + W
+        v.wait_ge(sem["ld%d" % k], 32)
+        v.quantize_mx(T.bc[:, a:b], T.bp[:, a:b], T.bt[:, 4 * a:4 * b]).then_inc(sem["bq%d" % k], 1)
+    v.wait_ge(sem.eye, 1)
+    for b in range(4):
+        v.quantize_mx(T.sc[:, W * b:W * b + W], T.sp[:, W * b:W * b + W], T.eye[:, 3 - b:3 - b + 4 * W]).then_inc(sem.sq, 1)
+    v.wait_ge(sem.ldx, 16)
+    v.quantize_mx(T.xc[:], T.xp[:], T.xt[:]).then_inc(sem.xq, 1)
+    for b in (0, 2):
+        v.wait_ge(sem["z%d" % b], 1)
+        v.tensor_scalar(T.ht[:, b:4 * W:4], T.zb[:, 512 * b:512 * b + W], 0.0, C2, AluOpType.max, AluOpType.mult).then_inc(sem.rv, 1)
+    v.wait_ge(sem.rv, 2)
+    v.wait_ge(sem.rs, 2)
+    v.quantize_mx(T.hc[:], T.hp[:], T.ht[:]).then_inc(sem.hq, 1)
+
+    g.wait_ge(sem.ones, 2)
+    g.affine_select(T.eye[:, 3:3 + 4 * W:4], T.one[:], [[-1, W]], AluOpType.is_equal, 0.0, 0, 1).then_inc(sem.eye, 1)
+    remote_calls(g, core, T, topo, steps)
+
+    t = g.tensor
+    t.wait_ge(sem.sq, 4)
+    t.wait_ge(sem[bq[me]], 1)
+    for i, r in enumerate(seq):
+        if i:
+            t.wait_ge(sem["a1_%d" % r], landed(steps, core, "a1_%d" % r))
+        c, p = (T.l1c, T.l1p) if i else (T.bc, T.bp)
+        for b in range(4):
+            m = t.matmul_mx(T.zb[:, 512 * b:512 * b + W], T.sc[:, W * b:W * b + W], T.sp[:, W * b:W * b + W],
+                            c[:, W * r:W * r + W], p[:, W * r:W * r + W], i == 0, i == N - 1)
+            if i == N - 1:
+                m.then_inc(sem["z%d" % b], 1)
+    t.wait_ge(sem.xq, 1)
+    t.wait_ge(sem.hq, 1)
+
+    def bank(i):
+        return T.yb[:, 512 * i:512 * i + NX] if i < 4 else T.zb[:, 512 * (i - 4):512 * (i - 4) + NX]
+
+    for i, r in enumerate(seq):
+        if i:
+            t.wait_ge(sem["a2_%d" % r], landed(steps, core, "a2_%d" % r))
+            c, p = T.l2c[:, W * r:W * r + W], T.l2p[:, W * r:W * r + W]
+        else:
+            c, p = T.hc[:], T.hp[:]
+        t.matmul_mx(bank(i), c, p, T.xc[:], T.xp[:], True, True).then_inc(sem["y%d" % i], 1)
+
+    a = g.scalar
+    for b in (1, 3):
+        a.wait_ge(sem["z%d" % b], 1)
+        a.activation(T.ht[:, b:4 * W:4], T.zb[:, 512 * b:512 * b + W], ActivationFunctionType.Relu, scale=C2).then_inc(sem.rs, 1)
+    g.sync.wait_ge(sem.rv, 2)
+    g.sync.wait_ge(sem.rs, 2)
+    g.sync.dma_start(T.h[:], T.ht[:]).then_inc(sem.st_y, 16)
+    ny = na = 0
+    for i, r in enumerate(seq):
+        o = T.yo[:, NX * r:NX * r + NX]
+        if i % 2:
+            v.wait_ge(sem["y%d" % i], 1)
+            v.tensor_copy(o, bank(i)).then_inc(sem["e%d" % i], 1)
+            g.sync.wait_ge(sem["e%d" % i], 1)
+            g.sync.dma_start(T.y[:, NX * r:NX * r + NX], o).then_inc(sem.st_y, 16)
+            ny += 16
+        else:
+            a.wait_ge(sem["y%d" % i], 1)
+            a.activation(o, bank(i), ActivationFunctionType.Copy).then_inc(sem["e%d" % i], 1)
+            a.wait_ge(sem["e%d" % i], 1)
+            a.dma_start(T.y[:, NX * r:NX * r + NX], o).then_inc(sem.st_a, 16)
+            na += 16
+    g.sync.wait_ge(sem.st_y, 16 + ny)
+    a.wait_ge(sem.st_a, na)

@@ -23,8 +23,8 @@ SCRATCH = {
     "l1p": ("sbuf", [128, N * W], "uint8"),
     "l2c": ("sbuf", [128, N * W], CODES),
     "l2p": ("sbuf", [128, N * W], "uint8"),
-    "r1c": ("sbuf", [128, N * W], CODES),
-    "r1p": ("sbuf", [128, N * W], "uint8"),
+    "r1c": ("sbuf", [128, W], CODES),
+    "r1p": ("sbuf", [128, W], "uint8"),
     "r2c": ("sbuf", [128, W], CODES),
     "r2p": ("sbuf", [128, W], "uint8"),
     "ht": ("sbuf", [128, 4 * W], "bfloat16"),
@@ -44,31 +44,44 @@ def engines(mask):
     return [e for e in range(mask.bit_length()) if mask >> e & 1]
 
 
-def far(s, d, topo):
+def links(s, d, topo):
     a, b = topo.chip(s), topo.chip(d)
-    k = 0 if a == b else 1 if topo.mates(a, b) else 2 if topo.same_plane(a, b) else 3
-    return k + (0 if topo.may_write(s, d) else 4)
+    return 0 if a == b else 1 if topo.mates(a, b) else 2 if topo.same_plane(a, b) else 3
 
 
-def chip_groups(me, cores, topo):
-    out = []
-    for r, c in enumerate(cores):
-        if out and topo.chip(cores[out[-1][-1]]) == topo.chip(c):
-            out[-1].append(r)
-        else:
-            out.append([r])
-    return sorted(out, key=lambda q: 0 if me in q else -max(far(cores[me], cores[r], topo) for r in q))
+def relayed(s, d, cores, topo):
+    return not topo.may_write(s, d) or (links(s, d, topo) == 3 and any(topo.mates(topo.chip(s), topo.chip(c)) for c in cores))
+
+
+def far(s, d, cores, topo):
+    return links(s, d, topo) + (4 if relayed(s, d, cores, topo) else 0)
 
 
 def relays(s, cores, topo):
-    barred = [r for r, d in enumerate(cores) if d != s and not topo.may_write(s, d)]
-    if not barred:
-        return []
-    barred.sort(key=lambda r: (-far(s, cores[r], topo), r))
-    near = [h for h in range(SIM) if topo.chip(h) == topo.chip(s) and topo.die(h) == topo.die(s)
-            and h not in cores and all(topo.may_write(h, cores[r]) for r in barred)]
-    per = -(-len(barred) // len(near))
-    return [(h, barred[per * i:per * i + per]) for i, h in enumerate(near) if per * i < len(barred)]
+    taken = []
+    for r in sorted([r for r, d in enumerate(cores) if d != s and relayed(s, d, cores, topo)],
+                    key=lambda r: (links(s, cores[r], topo), r)):
+        ok = [h for h in range(SIM) if h not in cores and topo.die(h) == topo.die(s) and topo.may_write(h, cores[r])
+              and all(h != q for q, _ in taken)]
+        near = [h for h in ok if topo.chip(h) == topo.chip(s) and not topo.may_write(s, cores[r])]
+        away = [h for h in ok if topo.same_plane(topo.chip(s), topo.chip(h)) and topo.mates(topo.chip(h), topo.chip(cores[r]))]
+        taken.append(((near + away)[0], r))
+    return sorted(taken, key=lambda hr: (-links(s, hr[0], topo), hr[1]))
+
+
+def loads(me, cores, topo):
+    chips = []
+    for r, c in enumerate(cores):
+        if chips and topo.chip(cores[chips[-1][-1]]) == topo.chip(c):
+            chips[-1].append(r)
+        else:
+            chips.append([r])
+    chips.sort(key=lambda q: 0 if me in q else -max(far(cores[me], cores[r], cores, topo) for r in q))
+    single = len(relays(cores[me], cores, topo)) > 0
+    out = []
+    for q in chips:
+        out += [[r] for r in q] if q == chips[0] or (single and me not in q) else [q]
+    return out
 
 
 def plan(cores, topo):
@@ -79,58 +92,59 @@ def plan(cores, topo):
 
     for me, s in enumerate(cores):
         rel = relays(s, cores, topo)
-        served = [r for _, rs in rel for r in rs]
         peers = [r for r, d in enumerate(cores) if d != s and topo.chip(d) == topo.chip(s)]
-        direct = [r for r, d in enumerate(cores) if d != s and r not in served and r not in peers]
+        direct = sorted([r for r, d in enumerate(cores) if d != s and r not in peers and all(r != q for _, q in rel)],
+                        key=lambda r: (-links(s, cores[r], topo), r))
         out = engines(topo.mask(s, [d for d in cores if topo.chip(d) != topo.chip(s)][0]))
         here = [e for e in engines(topo.mask(s, cores[peers[0]])) if e not in out]
-        gs = chip_groups(me, cores, topo)
-        bq = {r: "bq%d" % k for k, q in enumerate(gs) for r in q}
+        ready = {r: "bq%d" % k for k, q in enumerate(loads(me, cores, topo)) for r in q}
 
-        def spread(ranks, en):
-            return [([r], cores[r], r, en[i::len(ranks)]) for i, r in enumerate(ranks)]
-
-        if rel:
-            first = [(rs, h, None, here[i::len(rel)]) for i, (h, rs) in enumerate(rel)]
-            rest = spread(direct, out) + spread(peers, here)
-        else:
-            first = spread(gs[0], out)
-            rest = spread([r for r in direct if r not in gs[0]], out) + spread(peers, here[::2])
-        for part in (first, rest):
-            for kind in "cp":
-                waits = sorted(set(bq[r] for rs, _, _, _ in part for r in rs))
+        items, turn = [], {True: 0, False: 0}
+        for h, r in rel + [(None, r) for r in direct]:
+            stays = h is not None and topo.chip(h) == topo.chip(s)
+            items.append((r, h, (here if stays else out)[turn[stays] % 2::2]))
+            turn[stays] += 1
+        to_peer = [(r, None, here[::2]) for r in peers]
+        sends = [items[:1], items[1:3], items[3:] + to_peer] if rel else [items[:2], items[2:] + to_peer]
+        for part in sends:
+            for kind in "pc":
                 tr = []
-                for rs, d, r, en in part:
-                    a, b = W * rs[0], W * rs[-1] + W
-                    if r is None:
-                        tr.append((("b" + kind, a, b), [(d, "r1" + kind, 0, b - a)], en, "r1" + kind))
+                for r, h, en in part:
+                    src = ("b" + kind, W * r, W * r + W)
+                    if h is None:
+                        tr.append((src, [(cores[r], "l1" + kind, W * me, W * me + W)], en, "a1_%d" % me))
                     else:
-                        tr.append((("b" + kind, a, b), [(d, "l1" + kind, W * me, W * me + W)], en, "a1_%d" % me))
-                call(s, waits, tr)
+                        tr.append((src, [(h, "r1" + kind, 0, W)], en, "r1" + kind))
+                call(s, sorted(set(ready[r] for r, _, _ in part)), tr)
+
+        on = [(h, [r]) for h, r in rel if topo.chip(h) == topo.chip(s)]
+        off = [(h, r) for h, r in rel if topo.chip(h) != topo.chip(s)]
+        off = [(off[0][0], [r for _, r in off])] if off else []
 
         def to(ranks, kind, en):
             return (("h" + kind, 0, W), [(cores[r], "l2" + kind, W * me, W * me + W) for r in ranks], en, "a2_%d" % me)
 
         for kind in "cp":
-            if rel:
-                tr = [(("h" + kind, 0, W), [(h, "r2" + kind, 0, W) for h, _ in rel], here, "r2" + kind)]
+            tr = []
+            if on:
+                tr.append((("h" + kind, 0, W), [(h, "r2" + kind, 0, W) for h, _ in on], here, "r2" + kind))
             else:
-                tr = [to(peers, kind, here[::2])]
+                tr.append(to(peers, kind, here[::2]))
+            if off:
+                tr.append((("h" + kind, 0, W), [(h, "r2" + kind, 0, W) for h, _ in off], out[::2] if direct else out, "r2" + kind))
             if direct:
-                tr.append(to(sorted(direct, key=lambda r: -far(s, cores[r], topo)), kind, out))
+                tr.append(to(direct, kind, out[1::2] if off else out))
             call(s, ["hq"], tr)
-        if rel:
+        if on:
             for kind in "cp":
                 call(s, ["hq"], [to(peers, kind, here)])
 
-        for h, rs in rel:
-            use = out if len(rs) > 1 else out[::2]
+        for h, r in rel:
+            for kind in "pc":
+                call(h, ["r1" + kind], [(("r1" + kind, 0, W), [(cores[r], "l1" + kind, W * me, W * me + W)], out, "a1_%d" % me)])
+        for h, rs in on + off:
             for kind in "cp":
-                call(h, ["r1" + kind], [(("r1" + kind, W * i, W * i + W), [(cores[r], "l1" + kind, W * me, W * me + W)],
-                                         use[i::len(rs)], "a1_%d" % me) for i, r in enumerate(rs)])
-            for kind in "cp":
-                call(h, ["r2" + kind], [(("r2" + kind, 0, W), [(cores[r], "l2" + kind, W * me, W * me + W) for r in rs],
-                                         use, "a2_%d" % me)])
+                call(h, ["r2" + kind], [(("r2" + kind, 0, W), [(cores[r], "l2" + kind, W * me, W * me + W) for r in rs], out, "a2_%d" % me)])
     return steps
 
 
@@ -170,13 +184,15 @@ def rank_program(g, core, T, topo):
         remote_calls(g, core, T, topo, steps)
         return
 
-    gs = chip_groups(me, cores, topo)
-    bq = {r: "bq%d" % k for k, q in enumerate(gs) for r in q}
-    order = sorted([r for r in range(N) if r != me], key=lambda r: (far(cores[r], core, topo), r))
-    seq = [me] + order
+    runs = loads(me, cores, topo)
+    mine = [k for k, q in enumerate(runs) if me in q][0]
+    others = [r for r in range(N) if r != me]
+    way = {r: far(cores[r], core, cores, topo) for r in others}
+    seq1 = [me] + sorted(others, key=lambda r: (way[r], r))
+    seq2 = [me] + sorted(others, key=lambda r: ((way[r] + 2) % 4 + way[r] // 4 * 4, r))
     sem = T.sem
 
-    for k, q in enumerate(gs):
+    for k, q in enumerate(runs):
         a, b = 4 * W * q[0], 4 * W * q[-1] + 4 * W
         g.sync.dma_start(T.bt[0:64, a:b], T.b[0:64, a:b]).then_inc(sem["ld%d" % k], 16)
         g.scalar.dma_start(T.bt[64:128, a:b], T.b[64:128, a:b]).then_inc(sem["ld%d" % k], 16)
@@ -185,7 +201,7 @@ def rank_program(g, core, T, topo):
     v = g.vector
     v.memset(T.one[:], 1.0).then_inc(sem.ones, 1)
     v.memset(T.eye[:], 0.0).then_inc(sem.ones, 1)
-    for k, q in enumerate(gs):
+    for k, q in enumerate(runs):
         a, b = W * q[0], W * q[-1] + W
         v.wait_ge(sem["ld%d" % k], 32)
         v.quantize_mx(T.bc[:, a:b], T.bp[:, a:b], T.bt[:, 4 * a:4 * b]).then_inc(sem["bq%d" % k], 1)
@@ -194,11 +210,11 @@ def rank_program(g, core, T, topo):
         v.quantize_mx(T.sc[:, W * b:W * b + W], T.sp[:, W * b:W * b + W], T.eye[:, 3 - b:3 - b + 4 * W]).then_inc(sem.sq, 1)
     v.wait_ge(sem.ldx, 16)
     v.quantize_mx(T.xc[:], T.xp[:], T.xt[:]).then_inc(sem.xq, 1)
-    for b in (0, 2):
+    for b in (1, 3):
         v.wait_ge(sem["z%d" % b], 1)
         v.tensor_scalar(T.ht[:, b:4 * W:4], T.zb[:, 512 * b:512 * b + W], 0.0, C2, AluOpType.max, AluOpType.mult).then_inc(sem.rv, 1)
-    v.wait_ge(sem.rv, 2)
     v.wait_ge(sem.rs, 2)
+    v.wait_ge(sem.rv, 2)
     v.quantize_mx(T.hc[:], T.hp[:], T.ht[:]).then_inc(sem.hq, 1)
 
     g.wait_ge(sem.ones, 2)
@@ -207,8 +223,8 @@ def rank_program(g, core, T, topo):
 
     t = g.tensor
     t.wait_ge(sem.sq, 4)
-    t.wait_ge(sem[bq[me]], 1)
-    for i, r in enumerate(seq):
+    t.wait_ge(sem["bq%d" % mine], 1)
+    for i, r in enumerate(seq1):
         if i:
             t.wait_ge(sem["a1_%d" % r], landed(steps, core, "a1_%d" % r))
         c, p = (T.l1c, T.l1p) if i else (T.bc, T.bp)
@@ -223,7 +239,7 @@ def rank_program(g, core, T, topo):
     def bank(i):
         return T.yb[:, 512 * i:512 * i + NX] if i < 4 else T.zb[:, 512 * (i - 4):512 * (i - 4) + NX]
 
-    for i, r in enumerate(seq):
+    for i, r in enumerate(seq2):
         if i:
             t.wait_ge(sem["a2_%d" % r], landed(steps, core, "a2_%d" % r))
             c, p = T.l2c[:, W * r:W * r + W], T.l2p[:, W * r:W * r + W]
@@ -232,14 +248,14 @@ def rank_program(g, core, T, topo):
         t.matmul_mx(bank(i), c, p, T.xc[:], T.xp[:], True, True).then_inc(sem["y%d" % i], 1)
 
     a = g.scalar
-    for b in (1, 3):
+    for b in (0, 2):
         a.wait_ge(sem["z%d" % b], 1)
         a.activation(T.ht[:, b:4 * W:4], T.zb[:, 512 * b:512 * b + W], ActivationFunctionType.Relu, scale=C2).then_inc(sem.rs, 1)
     g.sync.wait_ge(sem.rv, 2)
     g.sync.wait_ge(sem.rs, 2)
     g.sync.dma_start(T.h[:], T.ht[:]).then_inc(sem.st_y, 16)
     ny = na = 0
-    for i, r in enumerate(seq):
+    for i, r in enumerate(seq2):
         o = T.yo[:, NX * r:NX * r + NX]
         if i % 2:
             v.wait_ge(sem["y%d" % i], 1)

@@ -7,6 +7,7 @@ W = 128
 NX = 256
 C2 = 0.30933
 CODES = "float8_e4m3fn_x4"
+PIECES = 8
 
 SCRATCH = {
     "bt": ("sbuf", [128, N * 4 * W], "bfloat16"),
@@ -15,7 +16,6 @@ SCRATCH = {
     "bp": ("sbuf", [128, N * W], "uint8"),
     "xc": ("sbuf", [128, NX], CODES),
     "xp": ("sbuf", [128, NX], "uint8"),
-    "one": ("sbuf", [128, W], "bfloat16"),
     "eye": ("sbuf", [128, 4 * W + 4], "bfloat16"),
     "sc": ("sbuf", [128, 4 * W], CODES),
     "sp": ("sbuf", [128, 4 * W], "uint8"),
@@ -36,12 +36,16 @@ SCRATCH = {
 }
 SEMAPHORES = (["a1_%d" % r for r in range(N)] + ["a2_%d" % r for r in range(N)] + ["r1c", "r1p", "r2c", "r2p", "sent"]
               + ["ld%d" % k for k in range(N)] + ["bq%d" % k for k in range(N)] + ["ldx", "xq", "ones", "eye", "sq"]
-              + ["z%d" % b for b in range(4)] + ["rv", "rs", "hq"]
-              + ["y%d" % k for k in range(N)] + ["e%d" % k for k in range(N)] + ["st_y", "st_a"])
+              + ["as%d" % b for b in range(4)] + ["z%d" % b for b in range(4)] + ["rv", "rs", "hq"]
+              + ["y%d" % k for k in range(PIECES)] + ["e%d" % k for k in range(PIECES)] + ["st_y", "st_a"])
 
 
 def engines(mask):
     return [e for e in range(mask.bit_length()) if mask >> e & 1]
+
+
+def leaving(s, cores, topo):
+    return engines(topo.mask(s, [d for d in cores if topo.chip(d) != topo.chip(s)][0]))
 
 
 def links(s, d, topo):
@@ -69,6 +73,33 @@ def relays(s, cores, topo):
     return sorted(taken, key=lambda hr: (-links(s, hr[0], topo), hr[1]))
 
 
+def direct_to(s, cores, topo):
+    return sorted([r for r, d in enumerate(cores) if topo.chip(d) != topo.chip(s) and not relayed(s, d, cores, topo)],
+                  key=lambda r: (-links(s, cores[r], topo), r))
+
+
+def helpers(cores, topo):
+    busy = list(cores) + [h for s in cores for h, _ in relays(s, cores, topo)]
+    out = {}
+    for me, s in enumerate(cores):
+        if not relays(s, cores, topo):
+            ranks = direct_to(s, cores, topo)
+            ranks = ranks[len(ranks) // 2:]
+            out[me] = ([h for h in range(SIM) if h not in busy and topo.chip(h) == topo.chip(s) and topo.die(h) == topo.die(s)
+                        and all(topo.may_write(h, cores[r]) for r in ranks)][0], ranks)
+    return out
+
+
+def pickers(cores, topo):
+    out = {r: [] for r in range(N)}
+    for s in cores:
+        for h, r in relays(s, cores, topo):
+            out[r].append(h)
+    for h, _ in helpers(cores, topo).values():
+        out[min([r for r in range(N) if topo.may_write(h, cores[r])], key=lambda r: (len(out[r]), r))].append(h)
+    return out
+
+
 def loads(me, cores, topo):
     chips = []
     for r, c in enumerate(cores):
@@ -77,25 +108,29 @@ def loads(me, cores, topo):
         else:
             chips.append([r])
     chips.sort(key=lambda q: 0 if me in q else -max(far(cores[me], cores[r], cores, topo) for r in q))
-    single = len(relays(cores[me], cores, topo)) > 0
     out = []
     for q in chips:
-        out += [[r] for r in q] if q == chips[0] or (single and me not in q) else [q]
+        out += [q] if me in q else [[r] for r in q]
     return out
 
 
 def plan(cores, topo):
-    steps = {}
+    steps, due1, due2 = {}, {}, {}
 
     def call(core, waits, transfers):
         steps.setdefault(core, []).append((waits, transfers))
 
+    for r, hs in pickers(cores, topo).items():
+        for b, h in enumerate(hs):
+            for kind in "cp":
+                call(h, ["sq"], [(("s" + kind, W * b, W * b + W), [(cores[r], "s" + kind, W * b, W * b + W)],
+                                  leaving(h, cores, topo), "as%d" % b)])
+
     for me, s in enumerate(cores):
         rel = relays(s, cores, topo)
         peers = [r for r, d in enumerate(cores) if d != s and topo.chip(d) == topo.chip(s)]
-        direct = sorted([r for r, d in enumerate(cores) if d != s and r not in peers and all(r != q for _, q in rel)],
-                        key=lambda r: (-links(s, cores[r], topo), r))
-        out = engines(topo.mask(s, [d for d in cores if topo.chip(d) != topo.chip(s)][0]))
+        direct = direct_to(s, cores, topo)
+        out = leaving(s, cores, topo)
         here = [e for e in engines(topo.mask(s, cores[peers[0]])) if e not in out]
         ready = {r: "bq%d" % k for k, q in enumerate(loads(me, cores, topo)) for r in q}
 
@@ -104,9 +139,9 @@ def plan(cores, topo):
             stays = h is not None and topo.chip(h) == topo.chip(s)
             items.append((r, h, (here if stays else out)[turn[stays] % 2::2]))
             turn[stays] += 1
-        to_peer = [(r, None, here[::2]) for r in peers]
+        to_peer = [(r, None, here[::2] if rel else here) for r in peers]
         sends = [items[:1], items[1:3], items[3:] + to_peer] if rel else [items[:2], items[2:] + to_peer]
-        for part in sends:
+        for k, part in enumerate(sends):
             for kind in "pc":
                 tr = []
                 for r, h, en in part:
@@ -116,36 +151,50 @@ def plan(cores, topo):
                     else:
                         tr.append((src, [(h, "r1" + kind, 0, W)], en, "r1" + kind))
                 call(s, sorted(set(ready[r] for r, _, _ in part)), tr)
+            for r, h, _ in part:
+                due1[me, r] = (h is not None, k if rel else k + 1, links(s, cores[r], topo))
 
-        on = [(h, [r]) for h, r in rel if topo.chip(h) == topo.chip(s)]
-        off = [(h, r) for h, r in rel if topo.chip(h) != topo.chip(s)]
-        off = [(off[0][0], [r for _, r in off])] if off else []
+        on = {kind: [(h, [r]) for h, r in rel if topo.chip(h) == topo.chip(s)] for kind in "cp"}
+        away = [(h, r) for h, r in rel if topo.chip(h) != topo.chip(s)]
+        off = {kind: [(away[k % len(away)][0], [r for _, r in away])] if away else [] for k, kind in enumerate("cp")}
+        helped = me in helpers(cores, topo)
+        if helped:
+            on = {kind: [helpers(cores, topo)[me]] for kind in "cp"}
+            direct = [r for r in direct if r not in on["c"][0][1]]
+        for late, ranks in enumerate([peers, direct, [r for _, rs in on["c"] for r in rs], [r for _, r in away]]):
+            for r in ranks:
+                due2[me, r] = (4 if late == 3 else 3 if late == 2 and helped else late, links(s, cores[r], topo))
 
         def to(ranks, kind, en):
             return (("h" + kind, 0, W), [(cores[r], "l2" + kind, W * me, W * me + W) for r in ranks], en, "a2_%d" % me)
 
+        def via(hrs, kind, en):
+            return (("h" + kind, 0, W), [(h, "r2" + kind, 0, W) for h, _ in hrs], en, "r2" + kind)
+
         for kind in "cp":
             tr = []
-            if on:
-                tr.append((("h" + kind, 0, W), [(h, "r2" + kind, 0, W) for h, _ in on], here, "r2" + kind))
-            else:
-                tr.append(to(peers, kind, here[::2]))
-            if off:
-                tr.append((("h" + kind, 0, W), [(h, "r2" + kind, 0, W) for h, _ in off], out[::2] if direct else out, "r2" + kind))
-            if direct:
-                tr.append(to(direct, kind, out[1::2] if off else out))
+            if on[kind]:
+                tr.append(via(on[kind], kind, here))
+            if away:
+                tr.append(via(off[kind], kind, out))
+            elif direct:
+                tr.append(to(direct, kind, out))
             call(s, ["hq"], tr)
-        if on:
-            for kind in "cp":
-                call(s, ["hq"], [to(peers, kind, here)])
+        for kind in "cp":
+            tr = [to(peers, kind, here if on[kind] else here[::2])]
+            if away and direct:
+                tr.append(to(direct, kind, out))
+            call(s, ["hq"], tr)
 
         for h, r in rel:
             for kind in "pc":
-                call(h, ["r1" + kind], [(("r1" + kind, 0, W), [(cores[r], "l1" + kind, W * me, W * me + W)], out, "a1_%d" % me)])
-        for h, rs in on + off:
-            for kind in "cp":
-                call(h, ["r2" + kind], [(("r2" + kind, 0, W), [(cores[r], "l2" + kind, W * me, W * me + W) for r in rs], out, "a2_%d" % me)])
-    return steps
+                call(h, ["r1" + kind], [(("r1" + kind, 0, W), [(cores[r], "l1" + kind, W * me, W * me + W)],
+                                         leaving(h, cores, topo), "a1_%d" % me)])
+        for kind in "cp":
+            for h, rs in on[kind] + off[kind]:
+                call(h, ["r2" + kind], [(("r2" + kind, 0, W), [(cores[r], "l2" + kind, W * me, W * me + W) for r in rs],
+                                         leaving(h, cores, topo), "a2_%d" % me)])
+    return steps, due1, due2
 
 
 def landed(steps, core, sem):
@@ -176,59 +225,72 @@ def remote_calls(g, core, T, topo, steps):
 
 def rank_program(g, core, T, topo):
     cores = list(T.cores)
-    steps = plan(cores, topo)
+    steps, due1, due2 = plan(cores, topo)
     if core not in steps:
         return
     me = T.rank_of(core)
+    picks = pickers(cores, topo)
+    sem, v = T.sem, g.vector
+
+    def make():
+        v.memset(T.eye[:], 0.0).then_inc(sem.ones, 1)
+        g.wait_ge(sem.ones, 1)
+        diagonal = T.eye[:, 3:3 + 4 * W:4]
+        g.affine_select(diagonal, diagonal, [[-1, W]], AluOpType.not_equal, 1.0, 0, 1).then_inc(sem.eye, 1)
+
+    def pack(bs):
+        v.wait_ge(sem.eye, 1)
+        for b in bs:
+            v.quantize_mx(T.sc[:, W * b:W * b + W], T.sp[:, W * b:W * b + W], T.eye[:, 3 - b:3 - b + 4 * W]).then_inc(sem.sq, 1)
+
+    make()
     if me is None:
+        pack([hs.index(core) for hs in picks.values() if core in hs])
         remote_calls(g, core, T, topo, steps)
         return
 
+    got = list(range(len(picks[me])))
+    own = list(range(len(got), 4))
     runs = loads(me, cores, topo)
     mine = [k for k, q in enumerate(runs) if me in q][0]
     others = [r for r in range(N) if r != me]
-    way = {r: far(cores[r], core, cores, topo) for r in others}
-    seq1 = [me] + sorted(others, key=lambda r: (way[r], r))
-    seq2 = [me] + sorted(others, key=lambda r: ((way[r] + 2) % 4 + way[r] // 4 * 4, r))
-    sem = T.sem
+    seq1 = [me] + sorted(others, key=lambda r: (due1[r, me], r))
+    seq2 = [me] + sorted(others, key=lambda r: (due2[r, me], r))
+    first1, first2 = "a1_%d" % seq1[1], "a2_%d" % seq2[1]
 
     for k, q in enumerate(runs):
         a, b = 4 * W * q[0], 4 * W * q[-1] + 4 * W
         g.sync.dma_start(T.bt[0:64, a:b], T.b[0:64, a:b]).then_inc(sem["ld%d" % k], 16)
         g.scalar.dma_start(T.bt[64:128, a:b], T.b[64:128, a:b]).then_inc(sem["ld%d" % k], 16)
+    g.sync.wait_ge(sem[first1], landed(steps, core, first1))
     g.sync.dma_start(T.xt[:], T.x[:]).then_inc(sem.ldx, 16)
 
-    v = g.vector
-    v.memset(T.one[:], 1.0).then_inc(sem.ones, 1)
-    v.memset(T.eye[:], 0.0).then_inc(sem.ones, 1)
     for k, q in enumerate(runs):
         a, b = W * q[0], W * q[-1] + W
         v.wait_ge(sem["ld%d" % k], 32)
         v.quantize_mx(T.bc[:, a:b], T.bp[:, a:b], T.bt[:, 4 * a:4 * b]).then_inc(sem["bq%d" % k], 1)
-    v.wait_ge(sem.eye, 1)
-    for b in range(4):
-        v.quantize_mx(T.sc[:, W * b:W * b + W], T.sp[:, W * b:W * b + W], T.eye[:, 3 - b:3 - b + 4 * W]).then_inc(sem.sq, 1)
-    v.wait_ge(sem.ldx, 16)
-    v.quantize_mx(T.xc[:], T.xp[:], T.xt[:]).then_inc(sem.xq, 1)
+    pack(own)
     for b in (1, 3):
         v.wait_ge(sem["z%d" % b], 1)
         v.tensor_scalar(T.ht[:, b:4 * W:4], T.zb[:, 512 * b:512 * b + W], 0.0, C2, AluOpType.max, AluOpType.mult).then_inc(sem.rv, 1)
     v.wait_ge(sem.rs, 2)
     v.wait_ge(sem.rv, 2)
     v.quantize_mx(T.hc[:], T.hp[:], T.ht[:]).then_inc(sem.hq, 1)
+    v.wait_ge(sem.ldx, 16)
+    v.quantize_mx(T.xc[:], T.xp[:], T.xt[:]).then_inc(sem.xq, 1)
 
-    g.wait_ge(sem.ones, 2)
-    g.affine_select(T.eye[:, 3:3 + 4 * W:4], T.one[:], [[-1, W]], AluOpType.is_equal, 0.0, 0, 1).then_inc(sem.eye, 1)
     remote_calls(g, core, T, topo, steps)
 
     t = g.tensor
-    t.wait_ge(sem.sq, 4)
     t.wait_ge(sem["bq%d" % mine], 1)
+    t.wait_ge(sem.sq, len(own))
     for i, r in enumerate(seq1):
         if i:
             t.wait_ge(sem["a1_%d" % r], landed(steps, core, "a1_%d" % r))
         c, p = (T.l1c, T.l1p) if i else (T.bc, T.bp)
-        for b in range(4):
+        for b in range(4) if i else own + got:
+            if not i and b in got:
+                t.wait_ge(sem["as%d" % b], landed(steps, core, "as%d" % b))
             m = t.matmul_mx(T.zb[:, 512 * b:512 * b + W], T.sc[:, W * b:W * b + W], T.sp[:, W * b:W * b + W],
                             c[:, W * r:W * r + W], p[:, W * r:W * r + W], i == 0, i == N - 1)
             if i == N - 1:
@@ -236,16 +298,19 @@ def rank_program(g, core, T, topo):
     t.wait_ge(sem.xq, 1)
     t.wait_ge(sem.hq, 1)
 
-    def bank(i):
-        return T.yb[:, 512 * i:512 * i + NX] if i < 4 else T.zb[:, 512 * (i - 4):512 * (i - 4) + NX]
-
+    pieces = []
     for i, r in enumerate(seq2):
-        if i:
+        pieces += [(r, 0, NX)] if i < N - 2 else [(r, 0, NX // 2), (r, NX // 2, NX)]
+
+    def bank(k):
+        w = pieces[k][2] - pieces[k][1]
+        return T.yb[:, 512 * k:512 * k + w] if k < 4 else T.zb[:, 512 * (k - 4):512 * (k - 4) + w]
+
+    for k, (r, lo, hi) in enumerate(pieces):
+        c, p = (T.hc[:], T.hp[:]) if r == me else (T.l2c[:, W * r:W * r + W], T.l2p[:, W * r:W * r + W])
+        if r != me and lo == 0:
             t.wait_ge(sem["a2_%d" % r], landed(steps, core, "a2_%d" % r))
-            c, p = T.l2c[:, W * r:W * r + W], T.l2p[:, W * r:W * r + W]
-        else:
-            c, p = T.hc[:], T.hp[:]
-        t.matmul_mx(bank(i), c, p, T.xc[:], T.xp[:], True, True).then_inc(sem["y%d" % i], 1)
+        t.matmul_mx(bank(k), c, p, T.xc[:, lo:hi], T.xp[:, lo:hi], True, True).then_inc(sem["y%d" % k], 1)
 
     a = g.scalar
     for b in (0, 2):
@@ -253,21 +318,22 @@ def rank_program(g, core, T, topo):
         a.activation(T.ht[:, b:4 * W:4], T.zb[:, 512 * b:512 * b + W], ActivationFunctionType.Relu, scale=C2).then_inc(sem.rs, 1)
     g.sync.wait_ge(sem.rv, 2)
     g.sync.wait_ge(sem.rs, 2)
+    g.sync.wait_ge(sem[first2], landed(steps, core, first2))
     g.sync.dma_start(T.h[:], T.ht[:]).then_inc(sem.st_y, 16)
     ny = na = 0
-    for i, r in enumerate(seq2):
-        o = T.yo[:, NX * r:NX * r + NX]
-        if i % 2:
-            v.wait_ge(sem["y%d" % i], 1)
-            v.tensor_copy(o, bank(i)).then_inc(sem["e%d" % i], 1)
-            g.sync.wait_ge(sem["e%d" % i], 1)
-            g.sync.dma_start(T.y[:, NX * r:NX * r + NX], o).then_inc(sem.st_y, 16)
+    for k, (r, lo, hi) in enumerate(pieces):
+        o, y = T.yo[:, NX * r + lo:NX * r + hi], T.y[:, NX * r + lo:NX * r + hi]
+        if k % 2:
+            v.wait_ge(sem["y%d" % k], 1)
+            v.tensor_copy(o, bank(k)).then_inc(sem["e%d" % k], 1)
+            g.sync.wait_ge(sem["e%d" % k], 1)
+            g.sync.dma_start(y, o).then_inc(sem.st_y, 16)
             ny += 16
         else:
-            a.wait_ge(sem["y%d" % i], 1)
-            a.activation(o, bank(i), ActivationFunctionType.Copy).then_inc(sem["e%d" % i], 1)
-            a.wait_ge(sem["e%d" % i], 1)
-            a.dma_start(T.y[:, NX * r:NX * r + NX], o).then_inc(sem.st_a, 16)
+            a.wait_ge(sem["y%d" % k], 1)
+            a.activation(o, bank(k), ActivationFunctionType.Copy).then_inc(sem["e%d" % k], 1)
+            a.wait_ge(sem["e%d" % k], 1)
+            a.dma_start(y, o).then_inc(sem.st_a, 16)
             na += 16
     g.sync.wait_ge(sem.st_y, 16 + ny)
     a.wait_ge(sem.st_a, na)

from concourse.bass import DstId, RemoteDMATransfer
from concourse.mybir import dt, AluOpType, ActivationFunctionType

N = 6
SIM = 80
W = 128
NX = 256
C2 = 0.30933
CODES = "float8_e4m3fn_x4"
PIECES = 8

SCRATCH = {
    "bt": ("sbuf", [128, N * 4 * W], "bfloat16"),
    "xt": ("sbuf", [128, 4 * NX], "bfloat16"),
    "bc": ("sbuf", [128, N * W], CODES),
    "bp": ("sbuf", [128, N * W], "uint8"),
    "xc": ("sbuf", [128, NX], CODES),
    "xp": ("sbuf", [128, NX], "uint8"),
    "eye": ("sbuf", [128, 4 * W + 4], "bfloat16"),
    "sc": ("sbuf", [128, 4 * W], CODES),
    "sp": ("sbuf", [128, 4 * W], "uint8"),
    "l1c": ("sbuf", [128, N * W], CODES),
    "l1p": ("sbuf", [128, N * W], "uint8"),
    "l2c": ("sbuf", [128, N * W], CODES),
    "l2p": ("sbuf", [128, N * W], "uint8"),
    "r1c": ("sbuf", [128, W], CODES),
    "r1p": ("sbuf", [128, W], "uint8"),
    "r2c": ("sbuf", [128, W], CODES),
    "r2p": ("sbuf", [128, W], "uint8"),
    "ht": ("sbuf", [128, 4 * W], "bfloat16"),
    "hc": ("sbuf", [128, W], CODES),
    "hp": ("sbuf", [128, W], "uint8"),
    "yo": ("sbuf", [128, N * NX], "float32"),
    "zb": ("psum", [128, 2048], "float32"),
    "yb": ("psum", [128, 2048], "float32"),
}
SEMAPHORES = (["a1_%d" % r for r in range(N)] + ["a2_%d" % r for r in range(N)] + ["r1c", "r1p", "r2c", "r2p", "sent"]
              + ["ld%d" % k for k in range(N)] + ["bq%d" % k for k in range(N)] + ["ldx", "xq", "ones", "eye", "sq"]
              + ["as%d" % b for b in range(4)] + ["z%d" % b for b in range(4)] + ["rv", "rs", "hq"]
              + ["y%d" % k for k in range(PIECES)] + ["e%d" % k for k in range(PIECES)] + ["st_y", "st_a"])


def engines(mask):
    return [e for e in range(mask.bit_length()) if mask >> e & 1]


def leaving(s, cores, topo):
    return engines(topo.mask(s, [d for d in cores if topo.chip(d) != topo.chip(s)][0]))


def links(s, d, topo):
    a, b = topo.chip(s), topo.chip(d)
    return 0 if a == b else 1 if topo.mates(a, b) else 2 if topo.same_plane(a, b) else 3


def relayed(s, d, cores, topo):
    return not topo.may_write(s, d) or (links(s, d, topo) == 3 and any(topo.mates(topo.chip(s), topo.chip(c)) for c in cores))


def far(s, d, cores, topo):
    return links(s, d, topo) + (4 if relayed(s, d, cores, topo) else 0)


def relays(s, cores, topo):
    taken = []
    for r in sorted([r for r, d in enumerate(cores) if d != s and relayed(s, d, cores, topo)],
                    key=lambda r: (links(s, cores[r], topo), r)):
        ok = [h for h in range(SIM) if h not in cores and topo.die(h) == topo.die(s) and topo.may_write(h, cores[r])
              and all(h != q for q, _ in taken)]
        near = [h for h in ok if topo.chip(h) == topo.chip(s) and not topo.may_write(s, cores[r])]
        away = [h for h in ok if topo.same_plane(topo.chip(s), topo.chip(h)) and topo.mates(topo.chip(h), topo.chip(cores[r]))]
        taken.append(((near + away)[0], r))
    return sorted(taken, key=lambda hr: (-links(s, hr[0], topo), hr[1]))


def direct_to(s, cores, topo):
    return sorted([r for r, d in enumerate(cores) if topo.chip(d) != topo.chip(s) and not relayed(s, d, cores, topo)],
                  key=lambda r: (-links(s, cores[r], topo), r))


def helpers(cores, topo):
    busy = list(cores) + [h for s in cores for h, _ in relays(s, cores, topo)]
    out = {}
    for me, s in enumerate(cores):
        if not relays(s, cores, topo):
            ranks = direct_to(s, cores, topo)
            ranks = ranks[len(ranks) // 2:]
            out[me] = ([h for h in range(SIM) if h not in busy and topo.chip(h) == topo.chip(s) and topo.die(h) == topo.die(s)
                        and all(topo.may_write(h, cores[r]) for r in ranks)][0], ranks)
    return out


def pickers(cores, topo):
    out = {r: [] for r in range(N)}
    for s in cores:
        for h, r in relays(s, cores, topo):
            out[r].append(h)
    for h, _ in helpers(cores, topo).values():
        out[min([r for r in range(N) if topo.may_write(h, cores[r])], key=lambda r: (len(out[r]), r))].append(h)
    return out


def loads(me, cores, topo):
    chips = []
    for r, c in enumerate(cores):
        if chips and topo.chip(cores[chips[-1][-1]]) == topo.chip(c):
            chips[-1].append(r)
        else:
            chips.append([r])
    chips.sort(key=lambda q: 0 if me in q else -max(far(cores[me], cores[r], cores, topo) for r in q))
    out = []
    for q in chips:
        out += [q] if me in q else [[r] for r in q]
    return out


def plan(cores, topo):
    steps, due1, due2 = {}, {}, {}

    def call(core, waits, transfers):
        steps.setdefault(core, []).append((waits, transfers))

    for r, hs in pickers(cores, topo).items():
        for b, h in enumerate(hs):
            for kind in "cp":
                call(h, ["sq"], [(("s" + kind, W * b, W * b + W), [(cores[r], "s" + kind, W * b, W * b + W)],
                                  leaving(h, cores, topo), "as%d" % b)])

    for me, s in enumerate(cores):
        rel = relays(s, cores, topo)
        peers = [r for r, d in enumerate(cores) if d != s and topo.chip(d) == topo.chip(s)]
        direct = direct_to(s, cores, topo)
        out = leaving(s, cores, topo)
        here = [e for e in engines(topo.mask(s, cores[peers[0]])) if e not in out]
        ready = {r: "bq%d" % k for k, q in enumerate(loads(me, cores, topo)) for r in q}

        items, turn = [], {True: 0, False: 0}
        for h, r in rel + [(None, r) for r in direct]:
            stays = h is not None and topo.chip(h) == topo.chip(s)
            items.append((r, h, (here if stays else out)[turn[stays] % 2::2]))
            turn[stays] += 1
        to_peer = [(r, None, here[::2] if rel else here) for r in peers]
        sends = [items[:1], items[1:3], items[3:] + to_peer] if rel else [items[:2], items[2:] + to_peer]
        for k, part in enumerate(sends):
            for kind in "pc":
                tr = []
                for r, h, en in part:
                    src = ("b" + kind, W * r, W * r + W)
                    if h is None:
                        tr.append((src, [(cores[r], "l1" + kind, W * me, W * me + W)], en, "a1_%d" % me))
                    else:
                        tr.append((src, [(h, "r1" + kind, 0, W)], en, "r1" + kind))
                call(s, sorted(set(ready[r] for r, _, _ in part)), tr)
            for r, h, _ in part:
                due1[me, r] = (h is not None, k if rel else k + 1, links(s, cores[r], topo))

        on = {kind: [(h, [r]) for h, r in rel if topo.chip(h) == topo.chip(s)] for kind in "cp"}
        away = [(h, r) for h, r in rel if topo.chip(h) != topo.chip(s)]
        off = {kind: [(away[k % len(away)][0], [r for _, r in away])] if away else [] for k, kind in enumerate("cp")}
        helped = me in helpers(cores, topo)
        if helped:
            on = {kind: [helpers(cores, topo)[me]] for kind in "cp"}
            direct = [r for r in direct if r not in on["c"][0][1]]
        for late, ranks in enumerate([peers, direct, [r for _, rs in on["c"] for r in rs], [r for _, r in away]]):
            for r in ranks:
                due2[me, r] = (4 if late == 3 else 3 if late == 2 and helped else late, links(s, cores[r], topo))

        def to(ranks, kind, en):
            return (("h" + kind, 0, W), [(cores[r], "l2" + kind, W * me, W * me + W) for r in ranks], en, "a2_%d" % me)

        def via(hrs, kind, en):
            return (("h" + kind, 0, W), [(h, "r2" + kind, 0, W) for h, _ in hrs], en, "r2" + kind)

        for kind in "cp":
            tr = []
            if on[kind]:
                tr.append(via(on[kind], kind, here))
            if away:
                tr.append(via(off[kind], kind, out))
            elif direct:
                tr.append(to(direct, kind, out))
            call(s, ["hq"], tr)
        for kind in "cp":
            tr = [to(peers, kind, here if on[kind] else here[::2])]
            if away and direct:
                tr.append(to(direct, kind, out))
            call(s, ["hq"], tr)

        for h, r in rel:
            for kind in "pc":
                call(h, ["r1" + kind], [(("r1" + kind, 0, W), [(cores[r], "l1" + kind, W * me, W * me + W)],
                                         leaving(h, cores, topo), "a1_%d" % me)])
        for kind in "cp":
            for h, rs in on[kind] + off[kind]:
                call(h, ["r2" + kind], [(("r2" + kind, 0, W), [(cores[r], "l2" + kind, W * me, W * me + W) for r in rs],
                                         leaving(h, cores, topo), "a2_%d" % me)])
    return steps, due1, due2


def landed(steps, core, sem):
    return sum(len(en) for calls in steps.values() for _, tr in calls for _, dsts, en, name in tr
               for d in dsts if d[0] == core and name == sem)


def side(T, buf, a, b):
    ap = T[buf][:, a:b]
    return ap.bitcast(dt.uint8) if buf[-1] == "c" else ap


def remote_calls(g, core, T, topo, steps):
    total = 0
    for waits, tr in steps[core]:
        for w in waits:
            g.wait_ge(T.sem[w], landed(steps, core, w) if w[0] == "r" else 1)
        xs = []
        for (buf, a, b), dsts, en, name in tr:
            ids = [topo.addr(d[0]) for d in dsts]
            xs.append(RemoteDMATransfer(srcs=[side(T, buf, a, b)], dsts=[side(T, d[1], d[2], d[3]) for d in dsts],
                                        dst_ids=[DstId(rid=i[0], pnc=i[1]) for i in ids],
                                        dma_engine_mask=sum(1 << e for e in en), remote_sem=T.sem[name]))
            total += len(en)
        g.remote_dma_fused(xs, local_sem=T.sem.sent)
    g.wait_ge(T.sem.sent, total)


def rank_program(g, core, T, topo):
    cores = list(T.cores)
    steps, due1, due2 = plan(cores, topo)
    if core not in steps:
        return
    me = T.rank_of(core)
    picks = pickers(cores, topo)
    sem, v = T.sem, g.vector

    def make():
        v.memset(T.eye[:], 0.0).then_inc(sem.ones, 1)
        g.wait_ge(sem.ones, 1)
        diagonal = T.eye[:, 3:3 + 4 * W:4]
        g.affine_select(diagonal, diagonal, [[-1, W]], AluOpType.not_equal, 1.0, 0, 1).then_inc(sem.eye, 1)

    def pack(bs):
        v.wait_ge(sem.eye, 1)
        for b in bs:
            v.quantize_mx(T.sc[:, W * b:W * b + W], T.sp[:, W * b:W * b + W], T.eye[:, 3 - b:3 - b + 4 * W]).then_inc(sem.sq, 1)

    make()
    if me is None:
        pack([hs.index(core) for hs in picks.values() if core in hs])
        remote_calls(g, core, T, topo, steps)
        return

    got = list(range(len(picks[me])))
    own = list(range(len(got), 4))
    runs = loads(me, cores, topo)
    mine = [k for k, q in enumerate(runs) if me in q][0]
    others = [r for r in range(N) if r != me]
    seq1 = [me] + sorted(others, key=lambda r: (due1[r, me], r))
    seq2 = [me] + sorted(others, key=lambda r: (due2[r, me], r))
    first1, first2 = "a1_%d" % seq1[1], "a2_%d" % seq2[1]

    for k, q in enumerate(runs):
        a, b = 4 * W * q[0], 4 * W * q[-1] + 4 * W
        g.sync.dma_start(T.bt[0:64, a:b], T.b[0:64, a:b]).then_inc(sem["ld%d" % k], 16)
        g.scalar.dma_start(T.bt[64:128, a:b], T.b[64:128, a:b]).then_inc(sem["ld%d" % k], 16)
    g.sync.wait_ge(sem[first1], landed(steps, core, first1))
    g.sync.dma_start(T.xt[:], T.x[:]).then_inc(sem.ldx, 16)

    for k, q in enumerate(runs):
        a, b = W * q[0], W * q[-1] + W
        v.wait_ge(sem["ld%d" % k], 32)
        v.quantize_mx(T.bc[:, a:b], T.bp[:, a:b], T.bt[:, 4 * a:4 * b]).then_inc(sem["bq%d" % k], 1)
    pack(own)
    for b in (1, 3):
        v.wait_ge(sem["z%d" % b], 1)
        v.tensor_scalar(T.ht[:, b:4 * W:4], T.zb[:, 512 * b:512 * b + W], 0.0, C2, AluOpType.max, AluOpType.mult).then_inc(sem.rv, 1)
    v.wait_ge(sem.rs, 2)
    v.wait_ge(sem.rv, 2)
    v.quantize_mx(T.hc[:], T.hp[:], T.ht[:]).then_inc(sem.hq, 1)
    v.wait_ge(sem.ldx, 16)
    v.quantize_mx(T.xc[:], T.xp[:], T.xt[:]).then_inc(sem.xq, 1)

    remote_calls(g, core, T, topo, steps)

    t = g.tensor
    t.wait_ge(sem["bq%d" % mine], 1)
    t.wait_ge(sem.sq, len(own))
    for i, r in enumerate(seq1):
        if i:
            t.wait_ge(sem["a1_%d" % r], landed(steps, core, "a1_%d" % r))
        c, p = (T.l1c, T.l1p) if i else (T.bc, T.bp)
        for b in range(4) if i else own + got:
            if not i and b in got:
                t.wait_ge(sem["as%d" % b], landed(steps, core, "as%d" % b))
            m = t.matmul_mx(T.zb[:, 512 * b:512 * b + W], T.sc[:, W * b:W * b + W], T.sp[:, W * b:W * b + W],
                            c[:, W * r:W * r + W], p[:, W * r:W * r + W], i == 0, i == N - 1)
            if i == N - 1:
                m.then_inc(sem["z%d" % b], 1)
    t.wait_ge(sem.xq, 1)
    t.wait_ge(sem.hq, 1)

    pieces = []
    for i, r in enumerate(seq2):
        pieces += [(r, 0, NX)] if i < N - 2 else [(r, 0, NX // 2), (r, NX // 2, NX)]

    def bank(k):
        w = pieces[k][2] - pieces[k][1]
        return T.yb[:, 512 * k:512 * k + w] if k < 4 else T.zb[:, 512 * (k - 4):512 * (k - 4) + w]

    for k, (r, lo, hi) in enumerate(pieces):
        c, p = (T.hc[:], T.hp[:]) if r == me else (T.l2c[:, W * r:W * r + W], T.l2p[:, W * r:W * r + W])
        if r != me and lo == 0:
            t.wait_ge(sem["a2_%d" % r], landed(steps, core, "a2_%d" % r))
        t.matmul_mx(bank(k), c, p, T.xc[:, lo:hi], T.xp[:, lo:hi], True, True).then_inc(sem["y%d" % k], 1)

    a = g.scalar
    for b in (0, 2):
        a.wait_ge(sem["z%d" % b], 1)
        a.activation(T.ht[:, b:4 * W:4], T.zb[:, 512 * b:512 * b + W], ActivationFunctionType.Relu, scale=C2).then_inc(sem.rs, 1)
    g.sync.wait_ge(sem.rv, 2)
    g.sync.wait_ge(sem.rs, 2)
    g.sync.wait_ge(sem[first2], landed(steps, core, first2))
    g.sync.dma_start(T.h[:], T.ht[:]).then_inc(sem.st_y, 16)
    ny = na = 0
    for k, (r, lo, hi) in enumerate(pieces):
        o, y = T.yo[:, NX * r + lo:NX * r + hi], T.y[:, NX * r + lo:NX * r + hi]
        if k % 2:
            v.wait_ge(sem["y%d" % k], 1)
            v.tensor_copy(o, bank(k)).then_inc(sem["e%d" % k], 1)
            g.sync.wait_ge(sem["e%d" % k], 1)
            g.sync.dma_start(y, o).then_inc(sem.st_y, 16)
            ny += 16
        else:
            a.wait_ge(sem["y%d" % k], 1)
            a.activation(o, bank(k), ActivationFunctionType.Copy).then_inc(sem["e%d" % k], 1)
            a.wait_ge(sem["e%d" % k], 1)
            a.dma_start(y, o).then_inc(sem.st_a, 16)
            na += 16
    g.sync.wait_ge(sem.st_y, 16 + ny)
    a.wait_ge(sem.st_a, na)
